import numpy as np
import ml_dtypes


def mxq(x, axis, fmt="e4m3"):
    dtype, down = {"e4m3": (ml_dtypes.float8_e4m3fn, 7), "e5m2": (ml_dtypes.float8_e5m2, 14)}[fmt]
    v = np.moveaxis(np.asarray(x, np.float32).astype(ml_dtypes.bfloat16).astype(np.float64), axis, -1)
    blocks = v.reshape(v.shape[:-1] + (-1, 32))
    amax = np.abs(blocks).max(-1, keepdims=True)
    byte = np.maximum(np.where(amax > 0, np.frexp(amax)[1] - 1 + 127, 0) - down, 1)
    scale = np.exp2(byte - 127.0)
    codes = (blocks / scale).astype(np.float32).astype(dtype).astype(np.float64)
    return np.moveaxis((codes * scale).reshape(v.shape), -1, axis)


WIDE = False


def mx_kscale(k):
    if not WIDE:
        return np.ones(k)
    levels = np.array([10, -10, 5, -5, 0])
    if k % 512:
        return np.exp2(np.random.permutation(np.resize(levels, k // 32))).repeat(32)
    a = np.empty((k // 512, 16))
    for p in range(k // 512):
        a[p, :8] = np.random.permutation(np.resize(levels, 8))
        for g in range(8):
            far = levels[np.abs(levels - a[p, g]) >= 10]
            a[p, g + 8] = far[np.random.randint(len(far))]
    return np.exp2(a.ravel()).repeat(32)


def f64(x):
    return np.asarray(x).astype(np.float64)


def striped(idx):
    return np.tile(idx.reshape(-1, 16).T, (8, 1)).astype(np.uint16)


def unstriped(offs):
    return offs[:16].T.reshape(-1).astype(np.int64)


E2M1 = np.array([0.0, 0.5, 1.0, 1.5, 2.0, 3.0, 4.0, 6.0, -0.0, -0.5, -1.0, -1.5, -2.0, -3.0, -4.0, -6.0])


def pack_weight(w, fmt):
    k, n = w.shape
    w = f64(np.asarray(w, np.float32).astype(ml_dtypes.bfloat16)).reshape(k // 32, 32, n)
    amax = np.abs(w).max(1)
    if fmt == "e4m3":
        byte = np.frexp(amax)[1] - 1 + 127 - 7
    else:
        mant, ex = np.frexp(amax / 6.0)
        byte = np.where(mant > 0.5, ex, ex - 1) + 127
    byte = np.clip(np.where(amax > 0, byte, 1), 1, 254)
    scaled = (w * np.exp2(127.0 - byte)[:, None, :]).reshape(k, n).astype(np.float32)
    by_word = np.ascontiguousarray(scaled.reshape(k // 512, 128, 4, n).transpose(0, 1, 3, 2))
    if fmt == "e4m3":
        words = by_word.astype(ml_dtypes.float8_e4m3fn).view(np.uint8)
    else:
        c = by_word.astype(ml_dtypes.float4_e2m1fn).view(np.uint8) & 0xF
        words = (c[..., 0::2] | (c[..., 1::2] << 4)).reshape(k // 512, 128, 2 * n)
    return np.ascontiguousarray(words), np.ascontiguousarray(byte.astype(np.uint8).reshape(k // 512, 16, n))


def unpack_weight(words, scales, fmt):
    g, _, n = scales.shape
    words = np.ascontiguousarray(words).reshape(g, 128, n, -1)
    if fmt == "e4m3":
        vals = words.view(ml_dtypes.float8_e4m3fn).astype(np.float64)
    else:
        nib = np.empty((g, 128, n, 4), np.uint8)
        nib[..., 0::2] = words & 0xF
        nib[..., 1::2] = words >> 4
        vals = E2M1[nib]
    vals = vals * np.repeat(np.exp2(scales.astype(np.float64) - 127.0), 8, axis=1)[..., None]
    return vals.transpose(0, 1, 3, 2).reshape(g * 512, n)


def gelu(v):
    return 0.5 * v * (1.0 + np.tanh(np.sqrt(2.0 / np.pi) * (v + 0.044715 * v**3)))


K, T, S, H, T2, N = 1024, 2048, 512, 1024, 1024, 512

def setup_inputs():
    n = np.random.standard_normal
    s = mx_kscale(K)[:, None]
    u = mx_kscale(H)[:, None]
    tab_words, tab_scales = pack_weight(n((K, T)) * s, "e4m3")
    w1 = n((K, H)) / np.sqrt(K) / s / u.T
    c = np.random.uniform(0.7, 1.4, H) / u[:, 0] ** 2
    w4_words, w4_scales = pack_weight(n((H, N)) / np.sqrt(H) / u, "e2m1")
    return {
        "tab_words": tab_words, "tab_scales": tab_scales,
        "offs": striped(np.random.permutation(T)[:S]),
        "w1": w1.astype(np.float32), "c": c.astype(np.float32),
        "wgs": np.exp(0.3 * n((128, S))).astype(np.float32),
        "offs2": striped(np.random.permutation(T2)[:S]),
        "state": (n((H, T2)) * u).astype(np.float32),
        "w4_words": w4_words, "w4_scales": w4_scales,
    }

def reference(tab_words, tab_scales, offs, w1, c, wgs, offs2, state, w4_words, w4_scales):
    v = unpack_weight(tab_words, tab_scales, "e4m3")[:, unstriped(offs)]
    w4 = unpack_weight(w4_words, w4_scales, "e2m1")
    p = mxq(f64(w1), 0, "e4m3").T @ v
    h = p / (f64(c)[:, None] + p * p)
    page = np.zeros((H, T2))
    page[:, unstriped(offs2)] = np.tile(f64(wgs), (H // 128, 1)) * h
    z = f64(state) - page
    y = w4.T @ mxq(z, 0, "e4m3")
    return y * y

@@ -1,0 +1,302 @@
+from contextlib import ExitStack
+
+import concourse.mybir as mybir
+from concourse.masks import make_identity
+
+K, T, S, H, T2, N = 1024, 2048, 512, 1024, 1024, 512
+FLOPS = 2 * K * H * S + 2 * H * N * T2
+
+F32 = mybir.dt.float32
+BF16 = mybir.dt.bfloat16
+I32 = mybir.dt.int32
+U32 = mybir.dt.uint32
+U16 = mybir.dt.uint16
+U8 = mybir.dt.uint8
+FP8X4 = mybir.dt.float8_e4m3fn_x4
+FP4X4 = mybir.dt.float4_e2m1fn_x4
+ACT = mybir.ActivationFunctionType
+ALU = mybir.AluOpType
+
+P = 128
+PACK = 4
+K_PASS = P * PACK
+BANK = 512
+PASSES = 2
+ROW_TILES = H // P
+HALVES = T2 // BANK
+BLOCKS = BANK // P
+
+
+def tile_list_robot_contact_effort_kernel(
+    tc, tab_words, tab_scales, offs, w1, c, wgs, offs2, state, w4_words, w4_scales, out
+):
+    nc = tc.nc
+    with ExitStack() as ctx:
+        keep = ctx.enter_context(tc.tile_pool(name="keep", bufs=1))
+        ring = ctx.enter_context(tc.tile_pool(name="ring", bufs=2))
+        psum = ctx.enter_context(tc.psum_pool(name="psum", bufs=1))
+
+        offs_sb = keep.tile([P, S // 16], U16, name="offs_sb")
+        nc.sync.dma_start(offs_sb[:], offs)
+        tab_sc = keep.tile([P, T], U8, name="tab_sc", align_bytes=64)
+        nc.gpsimd.memset(tab_sc[:].bitcast(I32), 0)
+        for q in range(4):
+            nc.gpsimd.dma_start(
+                tab_sc[32 * q : 32 * q + 8, :].bitcast(I32), tab_scales[:, 4 * q : 4 * q + 4, :].bitcast(I32)
+            )
+        c_rows = keep.tile([P, P], F32, name="c_rows")
+        nc.vector.memset(c_rows[:], 1.0)
+        nc.gpsimd.dma_start(c_rows[0:ROW_TILES, :], c.rearrange("(g q) -> g q", q=P))
+        w1_raw = {}
+
+        def load_w1(g0, count):
+            raw = keep.tile([P, PASSES, PACK, count * P], F32, name="w1_raw%d" % g0)
+            for a in range(PASSES):
+                rows = w1[a * K_PASS : (a + 1) * K_PASS, g0 * P : (g0 + count) * P]
+                nc.sync.dma_start(raw[:, a], rows.rearrange("(p i) c -> p i c", i=PACK))
+            for j in range(count):
+                w1_raw[g0 + j] = raw[:, :, :, j * P : (j + 1) * P]
+
+        state_sb = {}
+
+        def load_state(g):
+            st = keep.tile([P, T2], F32, name="state%d" % g)
+            nc.sync.dma_start(st[:], state[g * P : (g + 1) * P, :])
+            state_sb[g] = st
+
+        load_w1(0, 1)
+        tab_w = []
+        for a in range(PASSES):
+            t = keep.tile([P, T], U32, name="tab_w%d" % a, align_bytes=64)
+            nc.sync.dma_start(t[:].bitcast(I32), tab_words[a].rearrange("p t i -> p (t i)").bitcast(I32))
+            tab_w.append(t)
+        load_w1(1, 1)
+        wgs_sb = keep.tile([P, S], F32, name="wgs_sb")
+        nc.sync.dma_start(wgs_sb[:], wgs)
+        offs2_sb = keep.tile([P, S // 16], U16, name="offs2_sb")
+        nc.sync.dma_start(offs2_sb[:], offs2)
+        load_w1(2, 1)
+        load_w1(3, 1)
+        load_state(0)
+        load_w1(4, 2)
+        load_state(1)
+        load_state(2)
+        load_w1(6, 2)
+        load_state(3)
+        w4_w = keep.tile([P, PASSES, 2 * N], U8, name="w4_w", align_bytes=64)
+        nc.sync.dma_start(w4_w[:].bitcast(I32), w4_words.rearrange("a p n -> p a n").bitcast(I32))
+        w4_sc = keep.tile([P, PASSES, N], U8, name="w4_sc", align_bytes=64)
+        nc.vector.memset(w4_sc[:].bitcast(I32), 0)
+        for q in range(4):
+            nc.sync.dma_start(
+                w4_sc[32 * q : 32 * q + 4].bitcast(I32),
+                w4_scales[:, 4 * q : 4 * q + 4, :].rearrange("a r n -> r a n").bitcast(I32),
+            )
+        for g in range(4, ROW_TILES):
+            load_state(g)
+
+        ident = keep.tile([P, P], F32, name="ident")
+        make_identity(nc, ident[:])
+        pages = []
+        for j in range(2):
+            page = keep.tile([P, T2], F32, name="page%d" % j)
+            nc.vector.memset(page[:], 0.0)
+            pages.append(page)
+
+        c_ps = psum.tile([P, P], F32, name="c_ps", tag="t2_0")
+        nc.tensor.transpose(c_ps[:], c_rows[:], ident[:])
+        s_col = keep.tile([P, ROW_TILES], F32, name="s_col")
+        nc.scalar.activation(s_col[:], c_ps[:, 0:ROW_TILES], ACT.Abs_reciprocal_sqrt)
+        neg_s2 = keep.tile([P, ROW_TILES], F32, name="neg_s2")
+        nc.vector.scalar_tensor_tensor(neg_s2[:], s_col[:], -1.0, s_col[:], ALU.mult, ALU.mult)
+        cs2 = keep.tile([P, ROW_TILES], F32, name="cs2")
+        nc.vector.scalar_tensor_tensor(cs2[:], c_ps[:, 0:ROW_TILES], -1.0, neg_s2[:], ALU.mult, ALU.mult)
+
+        v_w = []
+        v_sc = keep.tile([P, S], U8, name="v_sc", align_bytes=64)
+        for a in range(PASSES):
+            v = keep.tile([P, S], U32, name="v_w%d" % a, align_bytes=64)
+            v_w.append(v)
+        nc.vector.tensor_copy(v_w[0][:], tab_w[0][:].indirect(offs_sb[:]))
+        nc.vector.tensor_copy(v_sc[:], tab_sc[:].indirect(offs_sb[:]))
+        for part in range(2):
+            nc.vector.tensor_copy(
+                v_w[1][:, part * 256 : (part + 1) * 256], tab_w[1][:].indirect(offs_sb[:, part * 16 : (part + 1) * 16])
+            )
+
+        w1_q = {}
+
+        def quantise_w1(g):
+            tag = {0: "w1_bf0", 1: "tab_w1", 2: "root0", 3: "root1"}.get(g, "recip%d" % (g - 3))
+            grouped = keep.tile([P, PASSES * P * PACK], BF16, name="w1_bf", tag=tag, align_bytes=64)
+            dst = grouped[:].rearrange("p (a c j i) -> p a c i j", a=PASSES, j=4, i=PACK)
+            src = w1_raw[g].rearrange("p a i (c j) -> p a c i j", j=4)
+            if g < 2:
+                nc.vector.tensor_copy(dst, src)
+            else:
+                nc.scalar.copy(dst, src)
+            codes = keep.tile([P, PASSES * P], U32, name="w1_codes%d" % g, align_bytes=64)
+            scales = keep.tile([P, PASSES * P], U8, name="w1_scales%d" % g, align_bytes=64)
+            nc.vector.quantize_mx(out=codes[:].bitcast(FP8X4), scales=scales[:], in_=grouped[:])
+            w1_q[g] = (codes, scales)
+
+        neg_h = {}
+        z_turned = [keep.tile([P, T2 * PACK], BF16, name="z_turned%d" % a) for a in range(PASSES)]
+
+        def room_of(g):
+            a, quarter = divmod(g, PACK)
+            words = z_turned[a][:].bitcast(F32).rearrange("t (r m) -> t r m", m=P)
+            return words[:, :, 32 * quarter : 32 * (quarter + 1)]
+
+        def runs(ap):
+            return ap.rearrange("p (r m) -> p r m", m=32)
+
+        def response(g):
+            codes, scales = w1_q[g]
+            sq = ring.tile([P, S], F32, name="sq")
+            if g < 2:
+                root_tile = keep.tile([P, S], F32, name="root%d" % g, align_bytes=64)
+                root = runs(root_tile[:])
+            else:
+                root = room_of(g - 2)
+            if g < ROW_TILES - 1:
+                recip_tile = keep.tile([P, S], F32, name="recip%d" % g, align_bytes=64)
+                recip = runs(recip_tile[:])
+            else:
+                recip = room_of(g - 1)
+            nh = ring.tile([P, S], F32, name="nh")
+            parts = [("p0", 0, 256), ("t2_1", 256, 512)] if g == 0 else [("p%d" % (g % 2), 0, S)]
+            for tag, j0, j1 in parts:
+                p_ps = psum.tile([P, j1 - j0], F32, name="p_ps", tag=tag)
+                for a in range(PASSES):
+                    cols = slice(a * P, (a + 1) * P)
+                    nc.tensor.matmul_mx(
+                        out=p_ps[:],
+                        lhsT=codes[:, cols].bitcast(FP8X4),
+                        lhsT_scale=scales[:, cols],
+                        rhs=v_w[a][:, j0:j1].bitcast(FP8X4),
+                        rhs_scale=v_sc[4 * a : P, j0:j1],
+                        start=(a == 0),
+                        stop=(a == PASSES - 1),
+                    )
+                rows = slice(j0 // 32, j1 // 32)
+                nc.scalar.activation(sq[:, j0:j1], p_ps[:], ACT.Square, scale=s_col[:, g : g + 1])
+                nc.scalar.activation(root[:, rows], runs(sq[:, j0:j1]), ACT.Abs_reciprocal_sqrt, bias=cs2[:, g : g + 1])
+                nc.scalar.activation(recip[:, rows], root[:, rows], ACT.Square)
+                nc.vector.scalar_tensor_tensor(
+                    runs(nh[:, j0:j1]), runs(p_ps[:]), neg_s2[:, g : g + 1], recip[:, rows], ALU.mult, ALU.mult
+                )
+            neg_h[g] = (nh, parts)
+
+        sums = {}
+
+        def place(g):
+            page = pages[g % 2]
+            banks = []
+            for h in range(HALVES):
+                bank = psum.tile([P, BLOCKS, P], F32, name="sum_ps", tag="t1_%d" % (2 * (g % 2) + h))
+                for b in range(BLOCKS):
+                    cols = slice(h * BANK + b * P, h * BANK + (b + 1) * P)
+                    nc.tensor.matmul(
+                        bank[:, b, :], state_sb[g][:, cols], ident[:], start=(b == 0), stop=False, is_transpose=True
+                    )
+                banks.append(bank)
+            nh, parts = neg_h[g]
+            for tag, j0, j1 in parts:
+                nc.vector.tensor_tensor(
+                    page[:].indirect(offs2_sb[:, j0 // 16 : j1 // 16]), nh[:, j0:j1], wgs_sb[:, j0:j1], ALU.mult
+                )
+            for h in range(HALVES):
+                for b in range(BLOCKS):
+                    cols = slice(h * BANK + b * P, h * BANK + (b + 1) * P)
+                    nc.tensor.matmul(
+                        banks[h][:, b, :], page[:, cols], ident[:],
+                        start=False, stop=(b == BLOCKS - 1), is_transpose=True,
+                    )
+            sums[g] = banks
+
+        def round_sums(g):
+            a, quarter = divmod(g, PACK)
+            view = z_turned[a][:].rearrange("t (b u m e) -> t b u m e", u=2, m=P, e=2)
+            for h in range(HALVES):
+                copy = nc.vector.tensor_copy if (g == ROW_TILES - 1 and h == 1) else nc.scalar.copy
+                copy(
+                    view[:, h * BLOCKS : (h + 1) * BLOCKS, :, 32 * quarter : 32 * (quarter + 1), :],
+                    sums[g][h][:].rearrange("t b (m u e) -> t b u m e", u=2, e=2),
+                )
+
+        z_q = {}
+
+        def quantise_z(a, h):
+            words = z_turned[a][:].bitcast(F32)[:, h * 2 * BANK : (h + 1) * 2 * BANK]
+            grouped = keep.tile([P, BANK * PACK], BF16, name="z_bf%d_%d" % (a, h), align_bytes=64)
+            pairs = grouped[:].bitcast(F32).rearrange("p (b t u) -> p b t u", t=P, u=2)
+            for j in range(2):
+                bank = psum.tile([P, 2, 2, P], F32, name="back_ps", tag="t2_%d" % j)
+                for b in range(2):
+                    for u in range(2):
+                        first = ((2 * j + b) * 2 + u) * P
+                        nc.tensor.transpose(bank[:, b, u, :], words[:, first : first + P], ident[:])
+                src = bank[:].rearrange("p b u t -> p b t u")
+                dst = pairs[:, 2 * j : 2 * j + 2]
+                if a == 1 and (h == 1 or j == 1):
+                    nc.vector.tensor_copy(dst, src)
+                else:
+                    nc.scalar.copy(dst, src)
+            codes = keep.tile([P, BANK], U32, name="z_codes%d_%d" % (a, h), align_bytes=64)
+            scales = keep.tile([P, BANK], U8, name="z_scales%d_%d" % (a, h), align_bytes=64)
+            nc.vector.quantize_mx(out=codes[:].bitcast(FP8X4), scales=scales[:], in_=grouped[:])
+            z_q[a, h] = (codes, scales)
+
+        y_ps = {}
+        y_tags = ["p0", "p1", "t1_0", "t1_1", "t1_2", "t1_3", "t2_0", "t2_1"]
+
+        def effort_pass(a, h, n):
+            if a == 0:
+                y_ps[h, n] = psum.tile([P, BANK], F32, name="y_ps", tag=y_tags[4 * h + n])
+            codes, scales = z_q[a, h]
+            nc.tensor.matmul_mx(
+                out=y_ps[h, n][:],
+                lhsT=w4_w[:, a, 2 * n * P : 2 * (n + 1) * P].bitcast(FP4X4),
+                lhsT_scale=w4_sc[:, a, n * P : (n + 1) * P],
+                rhs=codes[:].bitcast(FP8X4),
+                rhs_scale=scales[:],
+                start=(a == 0),
+                stop=(a == PASSES - 1),
+            )
+
+        def finish(h, n):
+            result = keep.tile([P, BANK], F32, name="result%d_%d" % (h, n))
+            nc.scalar.activation(result[:], y_ps[h, n][:], ACT.Square)
+            nc.sync.dma_start(out[n * P : (n + 1) * P, h * BANK : (h + 1) * BANK], result[:])
+
+        quantise_w1(0)
+        response(0)
+        quantise_w1(1)
+        response(1)
+        quantise_w1(2)
+        quantise_w1(3)
+        for g in range(ROW_TILES):
+            place(g)
+            if g + 2 < ROW_TILES:
+                response(g + 2)
+            round_sums(g)
+            if 1 <= g <= 4:
+                quantise_w1(g + 3)
+            if g == 3:
+                for h in range(HALVES):
+                    quantise_z(0, h)
+        for n in range(4):
+            effort_pass(0, 0, n)
+        quantise_z(1, 0)
+        for n in range(2):
+            effort_pass(0, 1, n)
+        quantise_z(1, 1)
+        for n in range(4):
+            effort_pass(1, 0, n)
+            finish(0, n)
+        for n in range(2, 4):
+            effort_pass(0, 1, n)
+        for n in range(4):
+            effort_pass(1, 1, n)
+            finish(1, n)

@@ -18,6 +18,12 @@ ACT = mybir.ActivationFunctionType
 ALU = mybir.AluOpType
 
 P = 128
+ROOM = 3
+ZT = ["root6", "root7"]
+FIRST = 1
+LAG = 1
+TB = 5
+SHIFT = 8
 PACK = 4
 K_PASS = P * PACK
 BANK = 512
@@ -36,26 +42,40 @@ def tile_list_robot_contact_effort_kernel(
         ring = ctx.enter_context(tc.tile_pool(name="ring", bufs=2))
         psum = ctx.enter_context(tc.psum_pool(name="psum", bufs=1))
 
-        offs_sb = keep.tile([P, S // 16], U16, name="offs_sb")
-        nc.sync.dma_start(offs_sb[:], offs)
-        tab_sc = keep.tile([P, T], U8, name="tab_sc", align_bytes=64)
-        nc.gpsimd.memset(tab_sc[:].bitcast(I32), 0)
-        for q in range(4):
-            nc.gpsimd.dma_start(
-                tab_sc[32 * q : 32 * q + 8, :].bitcast(I32), tab_scales[:, 4 * q : 4 * q + 4, :].bitcast(I32)
-            )
         c_rows = keep.tile([P, P], F32, name="c_rows")
-        nc.vector.memset(c_rows[:], 1.0)
-        nc.gpsimd.dma_start(c_rows[0:ROW_TILES, :], c.rearrange("(g q) -> g q", q=P))
+        tab_sc = keep.tile([P, T], U8, name="tab_sc", align_bytes=64)
+        offs_sb = keep.tile([P, S // 16], U16, name="offs_sb")
+
+        def load_small():
+            nc.gpsimd.memset(c_rows[:], 1.0)
+            nc.sync.dma_start(c_rows[0:ROW_TILES, :], c.rearrange("(g q) -> g q", q=P))
+            nc.vector.memset(tab_sc[:].bitcast(I32), 0)
+            for q in range(4):
+                nc.sync.dma_start(
+                    tab_sc[32 * q : 32 * q + 8, :].bitcast(I32), tab_scales[:, 4 * q : 4 * q + 4, :].bitcast(I32)
+                )
+            nc.sync.dma_start(offs_sb[:], offs)
+
+        tab_w = []
+
+        def load_table(a):
+            t = keep.tile([P, T], U32, name="tab_w%d" % a, align_bytes=64)
+            nc.sync.dma_start(t[:].bitcast(I32), tab_words[a].rearrange("p t i -> p (t i)").bitcast(I32))
+            tab_w.append(t)
+
         w1_raw = {}
 
         def load_w1(g0, count):
             raw = keep.tile([P, PASSES, PACK, count * P], F32, name="w1_raw%d" % g0)
+            for j in range(count):
+                w1_raw[g0 + j] = raw[:, :, :, j * P : (j + 1) * P]
             for a in range(PASSES):
                 rows = w1[a * K_PASS : (a + 1) * K_PASS, g0 * P : (g0 + count) * P]
                 nc.sync.dma_start(raw[:, a], rows.rearrange("(p i) c -> p i c", i=PACK))
-            for j in range(count):
-                w1_raw[g0 + j] = raw[:, :, :, j * P : (j + 1) * P]
+                if g0 == 0:
+                    if a == 0:
+                        load_small()
+                    load_table(a)
 
         state_sb = {}
 
@@ -64,24 +84,18 @@ def tile_list_robot_contact_effort_kernel(
             nc.sync.dma_start(st[:], state[g * P : (g + 1) * P, :])
             state_sb[g] = st
 
-        load_w1(0, 1)
-        tab_w = []
-        for a in range(PASSES):
-            t = keep.tile([P, T], U32, name="tab_w%d" % a, align_bytes=64)
-            nc.sync.dma_start(t[:].bitcast(I32), tab_words[a].rearrange("p t i -> p (t i)").bitcast(I32))
-            tab_w.append(t)
-        load_w1(1, 1)
+        load_w1(0, 2)
+        load_w1(2, 1)
         wgs_sb = keep.tile([P, S], F32, name="wgs_sb")
         nc.sync.dma_start(wgs_sb[:], wgs)
         offs2_sb = keep.tile([P, S // 16], U16, name="offs2_sb")
         nc.sync.dma_start(offs2_sb[:], offs2)
-        load_w1(2, 1)
         load_w1(3, 1)
         load_state(0)
         load_w1(4, 2)
         load_state(1)
-        load_state(2)
         load_w1(6, 2)
+        load_state(2)
         load_state(3)
         w4_w = keep.tile([P, PASSES, 2 * N], U8, name="w4_w", align_bytes=64)
         nc.sync.dma_start(w4_w[:].bitcast(I32), w4_words.rearrange("a p n -> p a n").bitcast(I32))
@@ -100,7 +114,7 @@ def tile_list_robot_contact_effort_kernel(
         pages = []
         for j in range(2):
             page = keep.tile([P, T2], F32, name="page%d" % j)
-            nc.vector.memset(page[:], 0.0)
+            nc.gpsimd.memset(page[:], 0.0)
             pages.append(page)
 
         c_ps = psum.tile([P, P], F32, name="c_ps", tag="t2_0")
@@ -117,8 +131,8 @@ def tile_list_robot_contact_effort_kernel(
         for a in range(PASSES):
             v = keep.tile([P, S], U32, name="v_w%d" % a, align_bytes=64)
             v_w.append(v)
-        nc.vector.tensor_copy(v_w[0][:], tab_w[0][:].indirect(offs_sb[:]))
         nc.vector.tensor_copy(v_sc[:], tab_sc[:].indirect(offs_sb[:]))
+        nc.vector.tensor_copy(v_w[0][:], tab_w[0][:].indirect(offs_sb[:]))
         for part in range(2):
             nc.vector.tensor_copy(
                 v_w[1][:, part * 256 : (part + 1) * 256], tab_w[1][:].indirect(offs_sb[:, part * 16 : (part + 1) * 16])
@@ -126,21 +140,25 @@ def tile_list_robot_contact_effort_kernel(
 
         w1_q = {}
 
-        def quantise_w1(g):
-            tag = {0: "w1_bf0", 1: "tab_w1", 2: "root0", 3: "root1"}.get(g, "recip%d" % (g - 3))
-            grouped = keep.tile([P, PASSES * P * PACK], BF16, name="w1_bf", tag=tag, align_bytes=64)
+        w1_bf = {}
+
+        def round_w1(g):
+            grouped = keep.tile([P, PASSES * P * PACK], BF16, name="w1_bf%d" % g, align_bytes=64)
             dst = grouped[:].rearrange("p (a c j i) -> p a c i j", a=PASSES, j=4, i=PACK)
             src = w1_raw[g].rearrange("p a i (c j) -> p a c i j", j=4)
-            if g < 2:
+            if g in (0, 2):
                 nc.vector.tensor_copy(dst, src)
             else:
                 nc.scalar.copy(dst, src)
-            codes = keep.tile([P, PASSES * P], U32, name="w1_codes%d" % g, align_bytes=64)
+            w1_bf[g] = grouped
+
+        def quantise_w1(g):
+            tag = "root%d" % (g - 2) if g >= FIRST + 2 else "w1_codes%d" % g
+            codes = keep.tile([P, PASSES * P], U32, name="w1_codes%d" % g, tag=tag, align_bytes=64)
             scales = keep.tile([P, PASSES * P], U8, name="w1_scales%d" % g, align_bytes=64)
-            nc.vector.quantize_mx(out=codes[:].bitcast(FP8X4), scales=scales[:], in_=grouped[:])
+            nc.vector.quantize_mx(out=codes[:].bitcast(FP8X4), scales=scales[:], in_=w1_bf[g][:])
             w1_q[g] = (codes, scales)
 
-        neg_h = {}
         z_turned = [keep.tile([P, T2 * PACK], BF16, name="z_turned%d" % a) for a in range(PASSES)]
 
         def room_of(g):
@@ -148,30 +166,46 @@ def tile_list_robot_contact_effort_kernel(
             words = z_turned[a][:].bitcast(F32).rearrange("t (r m) -> t r m", m=P)
             return words[:, :, 32 * quarter : 32 * (quarter + 1)]
 
-        def runs(ap):
-            return ap.rearrange("p (r m) -> p r m", m=32)
+        def runs(ap, length=32):
+            return ap.rearrange("p (r m) -> p r m", m=length)
+
+        def parts_of(g):
+            return [("p0", 0, S // 2), ("t2_1", S // 2, S)] if g == 0 else [("p%d" % ((g + (g >= SHIFT)) % 2), 0, S)]
+
+        p_ps, recips, neg_h, sums = {}, {}, {}, {}
+        first = keep.tile([P, 2 * S], F32, name="first")
 
         def response(g):
             codes, scales = w1_q[g]
-            sq = ring.tile([P, S], F32, name="sq")
-            if g < 2:
-                root_tile = keep.tile([P, S], F32, name="root%d" % g, align_bytes=64)
-                root = runs(root_tile[:])
+            ahead = g + 2 if FIRST <= g < ROW_TILES - 2 else None
+            if g == 0:
+                root_of = {0: first[:, 128:384], S // 2: first[:, 768:1024]}
+                sq_tile = keep.tile([P, S // 2], F32, name="sq0")
+                sq_of = {0: runs(sq_tile[:]), S // 2: runs(first[:, 0:256])}
             else:
-                root = room_of(g - 2)
-            if g < ROW_TILES - 1:
-                recip_tile = keep.tile([P, S], F32, name="recip%d" % g, align_bytes=64)
+                root_tile = keep.tile([P, S], F32, name="root%d" % g, align_bytes=64)
+                root_of = {0: root_tile[:]}
+                if g == 1:
+                    sq_of = {0: runs(first[:, 256:768])}
+                elif g < ROOM:
+                    sq_tile = keep.tile([P, S], F32, name="sq%d" % g, tag="recip0")
+                    sq_of = {0: runs(sq_tile[:])}
+                else:
+                    sq_of = {0: room_of(g - ROOM)}
+            if ahead:
+                recip = w1_raw[ahead][:, 0]
+            elif g < ROW_TILES - 1:
+                recip_tile = keep.tile([P, S], F32, name="recip%d" % g)
                 recip = runs(recip_tile[:])
             else:
                 recip = room_of(g - 1)
-            nh = ring.tile([P, S], F32, name="nh")
-            parts = [("p0", 0, 256), ("t2_1", 256, 512)] if g == 0 else [("p%d" % (g % 2), 0, S)]
-            for tag, j0, j1 in parts:
-                p_ps = psum.tile([P, j1 - j0], F32, name="p_ps", tag=tag)
+            for tag, j0, j1 in parts_of(g):
+                bank = psum.tile([P, j1 - j0], F32, name="p_ps", tag=tag)
+                p_ps[g, j0] = bank
                 for a in range(PASSES):
                     cols = slice(a * P, (a + 1) * P)
                     nc.tensor.matmul_mx(
-                        out=p_ps[:],
+                        out=bank[:],
                         lhsT=codes[:, cols].bitcast(FP8X4),
                         lhsT_scale=scales[:, cols],
                         rhs=v_w[a][:, j0:j1].bitcast(FP8X4),
@@ -180,76 +214,83 @@ def tile_list_robot_contact_effort_kernel(
                         stop=(a == PASSES - 1),
                     )
                 rows = slice(j0 // 32, j1 // 32)
-                nc.scalar.activation(sq[:, j0:j1], p_ps[:], ACT.Square, scale=s_col[:, g : g + 1])
-                nc.scalar.activation(root[:, rows], runs(sq[:, j0:j1]), ACT.Abs_reciprocal_sqrt, bias=cs2[:, g : g + 1])
-                nc.scalar.activation(recip[:, rows], root[:, rows], ACT.Square)
-                nc.vector.scalar_tensor_tensor(
-                    runs(nh[:, j0:j1]), runs(p_ps[:]), neg_s2[:, g : g + 1], recip[:, rows], ALU.mult, ALU.mult
-                )
-            neg_h[g] = (nh, parts)
+                nc.scalar.activation(sq_of[j0], runs(bank[:]), ACT.Square, scale=s_col[:, g : g + 1])
+                nc.scalar.activation(runs(root_of[j0]), sq_of[j0], ACT.Abs_reciprocal_sqrt, bias=cs2[:, g : g + 1])
+                if ahead:
+                    round_w1(ahead)
+                recips[g, j0] = recip[:, rows] if g == 0 else recip
+                nc.scalar.activation(recips[g, j0], runs(root_of[j0], recip.shape[2]), ACT.Square)
 
-        sums = {}
+        def weigh(g, part):
+            tag, j0, j1 = parts_of(g)[part]
+            nh = keep.tile([P, j1 - j0], F32, name="nh%d_%d" % (g, part))
+            recip = recips[g, j0]
+            length = recip.shape[2]
+            nc.vector.scalar_tensor_tensor(
+                runs(nh[:], length), runs(p_ps[g, j0][:], length), neg_s2[:, g : g + 1], recip, ALU.mult, ALU.mult
+            )
+            neg_h[g, part] = nh
 
-        def place(g):
-            page = pages[g % 2]
-            banks = []
-            for h in range(HALVES):
-                bank = psum.tile([P, BLOCKS, P], F32, name="sum_ps", tag="t1_%d" % (2 * (g % 2) + h))
-                for b in range(BLOCKS):
-                    cols = slice(h * BANK + b * P, h * BANK + (b + 1) * P)
+        def scatter(g, part):
+            tag, j0, j1 = parts_of(g)[part]
+            nc.vector.tensor_tensor(
+                pages[g % 2][:].indirect(offs2_sb[:, j0 // 16 : j1 // 16]), neg_h[g, part][:], wgs_sb[:, j0:j1], ALU.mult
+            )
+
+        def sum_tags(g):
+            if g < ROW_TILES - 1:
+                return ["t1_%d" % (2 * (g % 2) + h) for h in range(HALVES)]
+            return ["t1_2", "t1_3", "t2_0", "t2_1"]
+
+        def add_turned(g, source, opening):
+            blocks = T2 // P // len(sum_tags(g))
+            if opening:
+                sums[g] = [psum.tile([P, blocks, P], F32, name="sum_ps", tag=tag) for tag in sum_tags(g)]
+            for j, bank in enumerate(sums[g]):
+                for b in range(blocks):
+                    cols = slice((j * blocks + b) * P, (j * blocks + b + 1) * P)
                     nc.tensor.matmul(
-                        bank[:, b, :], state_sb[g][:, cols], ident[:], start=(b == 0), stop=False, is_transpose=True
+                        bank[:, b, :], source[:, cols], ident[:],
+                        start=(opening and b == 0), stop=(not opening and b == blocks - 1), is_transpose=True,
                     )
-                banks.append(bank)
-            nh, parts = neg_h[g]
-            for tag, j0, j1 in parts:
-                nc.vector.tensor_tensor(
-                    page[:].indirect(offs2_sb[:, j0 // 16 : j1 // 16]), nh[:, j0:j1], wgs_sb[:, j0:j1], ALU.mult
-                )
-            for h in range(HALVES):
-                for b in range(BLOCKS):
-                    cols = slice(h * BANK + b * P, h * BANK + (b + 1) * P)
-                    nc.tensor.matmul(
-                        banks[h][:, b, :], page[:, cols], ident[:],
-                        start=False, stop=(b == BLOCKS - 1), is_transpose=True,
-                    )
-            sums[g] = banks
 
         def round_sums(g):
             a, quarter = divmod(g, PACK)
             view = z_turned[a][:].rearrange("t (b u m e) -> t b u m e", u=2, m=P, e=2)
-            for h in range(HALVES):
-                copy = nc.vector.tensor_copy if (g == ROW_TILES - 1 and h == 1) else nc.scalar.copy
+            blocks = T2 // P // len(sums[g])
+            for j, bank in enumerate(sums[g]):
+                copy = nc.vector.tensor_copy if (g == ROW_TILES - 1 and j % 2 == 1) else nc.scalar.copy
                 copy(
-                    view[:, h * BLOCKS : (h + 1) * BLOCKS, :, 32 * quarter : 32 * (quarter + 1), :],
-                    sums[g][h][:].rearrange("t b (m u e) -> t b u m e", u=2, e=2),
+                    view[:, j * blocks : (j + 1) * blocks, :, 32 * quarter : 32 * (quarter + 1), :],
+                    bank[:].rearrange("t b (m u e) -> t b u m e", u=2, e=2),
                 )
 
-        z_q = {}
+        z_bf, z_q = {}, {}
 
-        def quantise_z(a, h):
+        def turn_back(a, h):
             words = z_turned[a][:].bitcast(F32)[:, h * 2 * BANK : (h + 1) * 2 * BANK]
-            grouped = keep.tile([P, BANK * PACK], BF16, name="z_bf%d_%d" % (a, h), align_bytes=64)
+            tag = ZT[h] if a == 0 else "z_bf%d" % h
+            grouped = keep.tile([P, BANK * PACK], BF16, name="z_bf%d_%d" % (a, h), tag=tag, align_bytes=64)
             pairs = grouped[:].bitcast(F32).rearrange("p (b t u) -> p b t u", t=P, u=2)
             for j in range(2):
-                bank = psum.tile([P, 2, 2, P], F32, name="back_ps", tag="t2_%d" % j)
+                tag = "t1_%d" % (2 * h + j) if a == 1 else "t2_%d" % j
+                bank = psum.tile([P, 2, 2, P], F32, name="back_ps", tag=tag)
                 for b in range(2):
                     for u in range(2):
                         first = ((2 * j + b) * 2 + u) * P
                         nc.tensor.transpose(bank[:, b, u, :], words[:, first : first + P], ident[:])
-                src = bank[:].rearrange("p b u t -> p b t u")
-                dst = pairs[:, 2 * j : 2 * j + 2]
-                if a == 1 and (h == 1 or j == 1):
-                    nc.vector.tensor_copy(dst, src)
-                else:
-                    nc.scalar.copy(dst, src)
+                copy = nc.vector.tensor_copy if (a == 1 and j == 1) else nc.scalar.copy
+                copy(pairs[:, 2 * j : 2 * j + 2], bank[:].rearrange("p b u t -> p b t u"))
+            z_bf[a, h] = grouped
+
+        def quantise_z(a, h):
             codes = keep.tile([P, BANK], U32, name="z_codes%d_%d" % (a, h), align_bytes=64)
             scales = keep.tile([P, BANK], U8, name="z_scales%d_%d" % (a, h), align_bytes=64)
-            nc.vector.quantize_mx(out=codes[:].bitcast(FP8X4), scales=scales[:], in_=grouped[:])
+            nc.vector.quantize_mx(out=codes[:].bitcast(FP8X4), scales=scales[:], in_=z_bf[a, h][:])
             z_q[a, h] = (codes, scales)
 
         y_ps = {}
-        y_tags = ["p0", "p1", "t1_0", "t1_1", "t1_2", "t1_3", "t2_0", "t2_1"]
+        y_tags = ["p%d" % (SHIFT < 8), "p%d" % (SHIFT == 8), "t2_0", "t2_1"] * 2
 
         def effort_pass(a, h, n):
             if a == 0:
@@ -270,33 +311,47 @@ def tile_list_robot_contact_effort_kernel(
             nc.scalar.activation(result[:], y_ps[h, n][:], ACT.Square)
             nc.sync.dma_start(out[n * P : (n + 1) * P, h * BANK : (h + 1) * BANK], result[:])
 
-        quantise_w1(0)
+        for g in range(3):
+            round_w1(g)
+            quantise_w1(g)
         response(0)
-        quantise_w1(1)
+        for part in range(2):
+            weigh(0, part)
+            scatter(0, part)
         response(1)
-        quantise_w1(2)
+        weigh(1, 0)
+        if FIRST == 2:
+            round_w1(2)
+            quantise_w1(2)
+        if FIRST == 2:
+            round_w1(3)
         quantise_w1(3)
         for g in range(ROW_TILES):
-            place(g)
+            if g > 0:
+                scatter(g, 0)
             if g + 2 < ROW_TILES:
                 response(g + 2)
+                weigh(g + 2, 0)
+            if g + 4 < ROW_TILES:
+                quantise_w1(g + 4)
+            if g >= LAG:
+                round_sums(g - LAG)
+            if g in (TB, TB + 1):
+                turn_back(0, g - TB)
+                quantise_z(0, g - TB)
+            if g == ROW_TILES - 1:
+                for n in range(2):
+                    effort_pass(0, 0, n)
+            add_turned(g, state_sb[g], True)
+            add_turned(g, pages[g % 2], False)
+        for g in range(ROW_TILES - LAG, ROW_TILES):
             round_sums(g)
-            if 1 <= g <= 4:
-                quantise_w1(g + 3)
-            if g == 3:
-                for h in range(HALVES):
-                    quantise_z(0, h)
-        for n in range(4):
-            effort_pass(0, 0, n)
-        quantise_z(1, 0)
-        for n in range(2):
-            effort_pass(0, 1, n)
-        quantise_z(1, 1)
-        for n in range(4):
-            effort_pass(1, 0, n)
-            finish(0, n)
-        for n in range(2, 4):
-            effort_pass(0, 1, n)
-        for n in range(4):
-            effort_pass(1, 1, n)
-            finish(1, n)
+        for h in range(HALVES):
+            turn_back(1, h)
+            quantise_z(1, h)
+        for h in range(HALVES):
+            for n in range(4):
+                if (h, n) not in y_ps:
+                    effort_pass(0, h, n)
+                effort_pass(1, h, n)
+                finish(h, n)

@@ -19,7 +19,7 @@ ALU = mybir.AluOpType
 
 P = 128
 ROOM = 3
-ZT = ["root6", "root7"]
+ZT = ["root6", "z_bf0_1"]
 FIRST = 1
 LAG = 1
 TB = 5
@@ -273,7 +273,7 @@ def tile_list_robot_contact_effort_kernel(
             grouped = keep.tile([P, BANK * PACK], BF16, name="z_bf%d_%d" % (a, h), tag=tag, align_bytes=64)
             pairs = grouped[:].bitcast(F32).rearrange("p (b t u) -> p b t u", t=P, u=2)
             for j in range(2):
-                tag = "t1_%d" % (2 * h + j) if a == 1 else "t2_%d" % j
+                tag = "t1_%d" % (2 + j) if (a, h) == (1, 0) else "t2_%d" % j
                 bank = psum.tile([P, 2, 2, P], F32, name="back_ps", tag=tag)
                 for b in range(2):
                     for u in range(2):
@@ -284,13 +284,14 @@ def tile_list_robot_contact_effort_kernel(
             z_bf[a, h] = grouped
 
         def quantise_z(a, h):
-            codes = keep.tile([P, BANK], U32, name="z_codes%d_%d" % (a, h), align_bytes=64)
+            tag = "root7" if (a, h) == (0, 0) else "z_codes%d_%d" % (a, h)
+            codes = keep.tile([P, BANK], U32, name="z_codes%d_%d" % (a, h), tag=tag, align_bytes=64)
             scales = keep.tile([P, BANK], U8, name="z_scales%d_%d" % (a, h), align_bytes=64)
             nc.vector.quantize_mx(out=codes[:].bitcast(FP8X4), scales=scales[:], in_=z_bf[a, h][:])
             z_q[a, h] = (codes, scales)
 
         y_ps = {}
-        y_tags = ["p%d" % (SHIFT < 8), "p%d" % (SHIFT == 8), "t2_0", "t2_1"] * 2
+        y_tags = ["p0", "p1", "t1_0", "t1_1"] * 2
 
         def effort_pass(a, h, n):
             if a == 0:
@@ -339,10 +340,10 @@ def tile_list_robot_contact_effort_kernel(
             if g in (TB, TB + 1):
                 turn_back(0, g - TB)
                 quantise_z(0, g - TB)
-            if g == ROW_TILES - 1:
-                for n in range(2):
-                    effort_pass(0, 0, n)
             add_turned(g, state_sb[g], True)
+            if g == ROW_TILES - 1:
+                for n in range(4):
+                    effort_pass(0, 0, n)
             add_turned(g, pages[g % 2], False)
         for g in range(ROW_TILES - LAG, ROW_TILES):
             round_sums(g)

@@ -18,19 +18,19 @@ ACT = mybir.ActivationFunctionType
 ALU = mybir.AluOpType
 
 P = 128
-ROOM = 3
-ZT = ["root6", "z_bf0_1"]
-FIRST = 1
-LAG = 1
-TB = 5
-SHIFT = 8
 PACK = 4
 K_PASS = P * PACK
-BANK = 512
 PASSES = 2
+BANK = 512
+QUADRANTS = 4
 ROW_TILES = H // P
+LAST = ROW_TILES - 1
 HALVES = T2 // BANK
 BLOCKS = BANK // P
+OUT_TILES = N // P
+RUN = P // PACK
+AHEAD = 2
+BEHIND = 3
 
 
 def tile_list_robot_contact_effort_kernel(
@@ -39,52 +39,52 @@ def tile_list_robot_contact_effort_kernel(
     nc = tc.nc
     with ExitStack() as ctx:
         keep = ctx.enter_context(tc.tile_pool(name="keep", bufs=1))
-        ring = ctx.enter_context(tc.tile_pool(name="ring", bufs=2))
         psum = ctx.enter_context(tc.psum_pool(name="psum", bufs=1))
+
+        w1_raw, tab_w, state_sb = {}, [], {}
+
+        def w1_tile(g0, count):
+            raw = keep.tile([P, PASSES, PACK, count * P], F32, name="w1_raw%d" % g0)
+            for j in range(count):
+                w1_raw[g0 + j] = raw[:, :, :, j * P : (j + 1) * P]
+            return raw
+
+        def load_w1_pass(raw, a, g0, count):
+            rows = w1[a * K_PASS : (a + 1) * K_PASS, g0 * P : (g0 + count) * P]
+            nc.sync.dma_start(raw[:, a], rows.rearrange("(p i) c -> p i c", i=PACK))
+
+        def load_w1(g0, count):
+            raw = w1_tile(g0, count)
+            for a in range(PASSES):
+                load_w1_pass(raw, a, g0, count)
+
+        def load_table(a):
+            words = keep.tile([P, T], U32, name="tab_w%d" % a, align_bytes=64)
+            nc.sync.dma_start(words[:].bitcast(I32), tab_words[a].rearrange("p t i -> p (t i)").bitcast(I32))
+            tab_w.append(words)
+
+        def load_state(g):
+            rows = keep.tile([P, T2], F32, name="state%d" % g)
+            nc.sync.dma_start(rows[:], state[g * P : (g + 1) * P, :])
+            state_sb[g] = rows
 
         c_rows = keep.tile([P, P], F32, name="c_rows")
         tab_sc = keep.tile([P, T], U8, name="tab_sc", align_bytes=64)
         offs_sb = keep.tile([P, S // 16], U16, name="offs_sb")
 
-        def load_small():
-            nc.gpsimd.memset(c_rows[:], 1.0)
-            nc.sync.dma_start(c_rows[0:ROW_TILES, :], c.rearrange("(g q) -> g q", q=P))
-            nc.vector.memset(tab_sc[:].bitcast(I32), 0)
-            for q in range(4):
-                nc.sync.dma_start(
-                    tab_sc[32 * q : 32 * q + 8, :].bitcast(I32), tab_scales[:, 4 * q : 4 * q + 4, :].bitcast(I32)
-                )
-            nc.sync.dma_start(offs_sb[:], offs)
-
-        tab_w = []
-
-        def load_table(a):
-            t = keep.tile([P, T], U32, name="tab_w%d" % a, align_bytes=64)
-            nc.sync.dma_start(t[:].bitcast(I32), tab_words[a].rearrange("p t i -> p (t i)").bitcast(I32))
-            tab_w.append(t)
-
-        w1_raw = {}
-
-        def load_w1(g0, count):
-            raw = keep.tile([P, PASSES, PACK, count * P], F32, name="w1_raw%d" % g0)
-            for j in range(count):
-                w1_raw[g0 + j] = raw[:, :, :, j * P : (j + 1) * P]
-            for a in range(PASSES):
-                rows = w1[a * K_PASS : (a + 1) * K_PASS, g0 * P : (g0 + count) * P]
-                nc.sync.dma_start(raw[:, a], rows.rearrange("(p i) c -> p i c", i=PACK))
-                if g0 == 0:
-                    if a == 0:
-                        load_small()
-                    load_table(a)
-
-        state_sb = {}
-
-        def load_state(g):
-            st = keep.tile([P, T2], F32, name="state%d" % g)
-            nc.sync.dma_start(st[:], state[g * P : (g + 1) * P, :])
-            state_sb[g] = st
-
-        load_w1(0, 2)
+        raw_first = w1_tile(0, 2)
+        load_w1_pass(raw_first, 0, 0, 2)
+        nc.gpsimd.memset(c_rows[:], 1.0)
+        nc.sync.dma_start(c_rows[0:ROW_TILES, :], c.rearrange("(g q) -> g q", q=P))
+        nc.vector.memset(tab_sc[:].bitcast(I32), 0)
+        for q in range(QUADRANTS):
+            nc.sync.dma_start(
+                tab_sc[32 * q : 32 * q + 4 * PASSES, :].bitcast(I32), tab_scales[:, 4 * q : 4 * q + 4, :].bitcast(I32)
+            )
+        nc.sync.dma_start(offs_sb[:], offs)
+        load_table(0)
+        load_w1_pass(raw_first, 1, 0, 2)
+        load_table(1)
         load_w1(2, 1)
         wgs_sb = keep.tile([P, S], F32, name="wgs_sb")
         nc.sync.dma_start(wgs_sb[:], wgs)
@@ -101,7 +101,7 @@ def tile_list_robot_contact_effort_kernel(
         nc.sync.dma_start(w4_w[:].bitcast(I32), w4_words.rearrange("a p n -> p a n").bitcast(I32))
         w4_sc = keep.tile([P, PASSES, N], U8, name="w4_sc", align_bytes=64)
         nc.vector.memset(w4_sc[:].bitcast(I32), 0)
-        for q in range(4):
+        for q in range(QUADRANTS):
             nc.sync.dma_start(
                 w4_sc[32 * q : 32 * q + 4].bitcast(I32),
                 w4_scales[:, 4 * q : 4 * q + 4, :].rearrange("a r n -> r a n").bitcast(I32),
@@ -117,7 +117,7 @@ def tile_list_robot_contact_effort_kernel(
             nc.gpsimd.memset(page[:], 0.0)
             pages.append(page)
 
-        c_ps = psum.tile([P, P], F32, name="c_ps", tag="t2_0")
+        c_ps = psum.tile([P, P], F32, name="c_ps", tag="back0")
         nc.tensor.transpose(c_ps[:], c_rows[:], ident[:])
         s_col = keep.tile([P, ROW_TILES], F32, name="s_col")
         nc.scalar.activation(s_col[:], c_ps[:, 0:ROW_TILES], ACT.Abs_reciprocal_sqrt)
@@ -126,34 +126,26 @@ def tile_list_robot_contact_effort_kernel(
         cs2 = keep.tile([P, ROW_TILES], F32, name="cs2")
         nc.vector.scalar_tensor_tensor(cs2[:], c_ps[:, 0:ROW_TILES], -1.0, neg_s2[:], ALU.mult, ALU.mult)
 
-        v_w = []
         v_sc = keep.tile([P, S], U8, name="v_sc", align_bytes=64)
-        for a in range(PASSES):
-            v = keep.tile([P, S], U32, name="v_w%d" % a, align_bytes=64)
-            v_w.append(v)
+        v_w = [keep.tile([P, S], U32, name="v_w%d" % a, align_bytes=64) for a in range(PASSES)]
         nc.vector.tensor_copy(v_sc[:], tab_sc[:].indirect(offs_sb[:]))
         nc.vector.tensor_copy(v_w[0][:], tab_w[0][:].indirect(offs_sb[:]))
-        for part in range(2):
-            nc.vector.tensor_copy(
-                v_w[1][:, part * 256 : (part + 1) * 256], tab_w[1][:].indirect(offs_sb[:, part * 16 : (part + 1) * 16])
-            )
+        for j0 in (0, S // 2):
+            j1 = j0 + S // 2
+            nc.vector.tensor_copy(v_w[1][:, j0:j1], tab_w[1][:].indirect(offs_sb[:, j0 // 16 : j1 // 16]))
 
-        w1_q = {}
-
-        w1_bf = {}
+        w1_bf, w1_q = {}, {}
 
         def round_w1(g):
             grouped = keep.tile([P, PASSES * P * PACK], BF16, name="w1_bf%d" % g, align_bytes=64)
             dst = grouped[:].rearrange("p (a c j i) -> p a c i j", a=PASSES, j=4, i=PACK)
             src = w1_raw[g].rearrange("p a i (c j) -> p a c i j", j=4)
-            if g in (0, 2):
-                nc.vector.tensor_copy(dst, src)
-            else:
-                nc.scalar.copy(dst, src)
+            copy = nc.vector.tensor_copy if g in (0, 2) else nc.scalar.copy
+            copy(dst, src)
             w1_bf[g] = grouped
 
         def quantise_w1(g):
-            tag = "root%d" % (g - 2) if g >= FIRST + 2 else "w1_codes%d" % g
+            tag = "root%d" % (g - AHEAD) if g > AHEAD else "w1_codes%d" % g
             codes = keep.tile([P, PASSES * P], U32, name="w1_codes%d" % g, tag=tag, align_bytes=64)
             scales = keep.tile([P, PASSES * P], U8, name="w1_scales%d" % g, align_bytes=64)
             nc.vector.quantize_mx(out=codes[:].bitcast(FP8X4), scales=scales[:], in_=w1_bf[g][:])
@@ -164,41 +156,43 @@ def tile_list_robot_contact_effort_kernel(
         def room_of(g):
             a, quarter = divmod(g, PACK)
             words = z_turned[a][:].bitcast(F32).rearrange("t (r m) -> t r m", m=P)
-            return words[:, :, 32 * quarter : 32 * (quarter + 1)]
+            return words[:, :, RUN * quarter : RUN * (quarter + 1)]
 
-        def runs(ap, length=32):
+        def runs(ap, length=RUN):
             return ap.rearrange("p (r m) -> p r m", m=length)
 
         def parts_of(g):
-            return [("p0", 0, S // 2), ("t2_1", S // 2, S)] if g == 0 else [("p%d" % ((g + (g >= SHIFT)) % 2), 0, S)]
+            if g == 0:
+                return [("p0", 0, S // 2), ("back1", S // 2, S)]
+            return [("p%d" % (g % 2), 0, S)]
 
         p_ps, recips, neg_h, sums = {}, {}, {}, {}
-        first = keep.tile([P, 2 * S], F32, name="first")
+        start_scratch = keep.tile([P, 2 * S], F32, name="start_scratch")
 
         def response(g):
             codes, scales = w1_q[g]
-            ahead = g + 2 if FIRST <= g < ROW_TILES - 2 else None
+            ahead = g + AHEAD if 0 < g < ROW_TILES - AHEAD else None
             if g == 0:
-                root_of = {0: first[:, 128:384], S // 2: first[:, 768:1024]}
+                root_of = {0: start_scratch[:, 128:384], S // 2: start_scratch[:, 768:1024]}
                 sq_tile = keep.tile([P, S // 2], F32, name="sq0")
-                sq_of = {0: runs(sq_tile[:]), S // 2: runs(first[:, 0:256])}
+                sq_of = {0: runs(sq_tile[:]), S // 2: runs(start_scratch[:, 0:256])}
             else:
                 root_tile = keep.tile([P, S], F32, name="root%d" % g, align_bytes=64)
                 root_of = {0: root_tile[:]}
                 if g == 1:
-                    sq_of = {0: runs(first[:, 256:768])}
-                elif g < ROOM:
+                    sq_of = {0: runs(start_scratch[:, 256:768])}
+                elif g < BEHIND:
                     sq_tile = keep.tile([P, S], F32, name="sq%d" % g, tag="recip0")
                     sq_of = {0: runs(sq_tile[:])}
                 else:
-                    sq_of = {0: room_of(g - ROOM)}
+                    sq_of = {0: room_of(g - BEHIND)}
             if ahead:
                 recip = w1_raw[ahead][:, 0]
-            elif g < ROW_TILES - 1:
+            elif g < LAST:
                 recip_tile = keep.tile([P, S], F32, name="recip%d" % g)
                 recip = runs(recip_tile[:])
             else:
-                recip = room_of(g - 1)
+                recip = room_of(LAST - 1)
             for tag, j0, j1 in parts_of(g):
                 bank = psum.tile([P, j1 - j0], F32, name="p_ps", tag=tag)
                 p_ps[g, j0] = bank
@@ -213,23 +207,22 @@ def tile_list_robot_contact_effort_kernel(
                         start=(a == 0),
                         stop=(a == PASSES - 1),
                     )
-                rows = slice(j0 // 32, j1 // 32)
                 nc.scalar.activation(sq_of[j0], runs(bank[:]), ACT.Square, scale=s_col[:, g : g + 1])
                 nc.scalar.activation(runs(root_of[j0]), sq_of[j0], ACT.Abs_reciprocal_sqrt, bias=cs2[:, g : g + 1])
                 if ahead:
                     round_w1(ahead)
-                recips[g, j0] = recip[:, rows] if g == 0 else recip
+                recips[g, j0] = recip[:, j0 // RUN : j1 // RUN] if g == 0 else recip
                 nc.scalar.activation(recips[g, j0], runs(root_of[j0], recip.shape[2]), ACT.Square)
 
         def weigh(g, part):
             tag, j0, j1 = parts_of(g)[part]
-            nh = keep.tile([P, j1 - j0], F32, name="nh%d_%d" % (g, part))
+            product = keep.tile([P, j1 - j0], F32, name="neg_h%d_%d" % (g, part))
             recip = recips[g, j0]
             length = recip.shape[2]
             nc.vector.scalar_tensor_tensor(
-                runs(nh[:], length), runs(p_ps[g, j0][:], length), neg_s2[:, g : g + 1], recip, ALU.mult, ALU.mult
+                runs(product[:], length), runs(p_ps[g, j0][:], length), neg_s2[:, g : g + 1], recip, ALU.mult, ALU.mult
             )
-            neg_h[g, part] = nh
+            neg_h[g, part] = product
 
         def scatter(g, part):
             tag, j0, j1 = parts_of(g)[part]
@@ -237,15 +230,11 @@ def tile_list_robot_contact_effort_kernel(
                 pages[g % 2][:].indirect(offs2_sb[:, j0 // 16 : j1 // 16]), neg_h[g, part][:], wgs_sb[:, j0:j1], ALU.mult
             )
 
-        def sum_tags(g):
-            if g < ROW_TILES - 1:
-                return ["t1_%d" % (2 * (g % 2) + h) for h in range(HALVES)]
-            return ["t1_2", "t1_3", "t2_0", "t2_1"]
-
         def add_turned(g, source, opening):
-            blocks = T2 // P // len(sum_tags(g))
             if opening:
-                sums[g] = [psum.tile([P, blocks, P], F32, name="sum_ps", tag=tag) for tag in sum_tags(g)]
+                tags = ["sum%d" % (2 * (g % 2) + h) for h in range(HALVES)] + (["back0", "back1"] if g == LAST else [])
+                sums[g] = [psum.tile([P, T2 // P // len(tags), P], F32, name="sum_ps", tag=tag) for tag in tags]
+            blocks = T2 // P // len(sums[g])
             for j, bank in enumerate(sums[g]):
                 for b in range(blocks):
                     cols = slice((j * blocks + b) * P, (j * blocks + b + 1) * P)
@@ -259,43 +248,55 @@ def tile_list_robot_contact_effort_kernel(
             view = z_turned[a][:].rearrange("t (b u m e) -> t b u m e", u=2, m=P, e=2)
             blocks = T2 // P // len(sums[g])
             for j, bank in enumerate(sums[g]):
-                copy = nc.vector.tensor_copy if (g == ROW_TILES - 1 and j % 2 == 1) else nc.scalar.copy
+                copy = nc.vector.tensor_copy if (g == LAST and j % 2 == 1) else nc.scalar.copy
                 copy(
-                    view[:, j * blocks : (j + 1) * blocks, :, 32 * quarter : 32 * (quarter + 1), :],
+                    view[:, j * blocks : (j + 1) * blocks, :, RUN * quarter : RUN * (quarter + 1), :],
                     bank[:].rearrange("t b (m u e) -> t b u m e", u=2, e=2),
                 )
 
         z_bf, z_q = {}, {}
+        back_tags = {
+            (0, 0): ["back0", "back1"],
+            (0, 1): ["back0", "back1"],
+            (1, 0): ["sum2", "sum3", "back0", "back1"],
+            (1, 1): ["sum2", "sum3"],
+        }
 
         def turn_back(a, h):
             words = z_turned[a][:].bitcast(F32)[:, h * 2 * BANK : (h + 1) * 2 * BANK]
-            tag = ZT[h] if a == 0 else "z_bf%d" % h
+            tag = "root%d" % (LAST - 1) if (a, h) == (0, 0) else "z_bf%d_%d" % (a, h)
             grouped = keep.tile([P, BANK * PACK], BF16, name="z_bf%d_%d" % (a, h), tag=tag, align_bytes=64)
             pairs = grouped[:].bitcast(F32).rearrange("p (b t u) -> p b t u", t=P, u=2)
-            for j in range(2):
-                tag = "t1_%d" % (2 + j) if (a, h) == (1, 0) else "t2_%d" % j
-                bank = psum.tile([P, 2, 2, P], F32, name="back_ps", tag=tag)
-                for b in range(2):
+            blocks = BLOCKS // len(back_tags[a, h])
+            for j, tag in enumerate(back_tags[a, h]):
+                bank = psum.tile([P, blocks, 2, P], F32, name="back_ps", tag=tag)
+                for b in range(blocks):
                     for u in range(2):
-                        first = ((2 * j + b) * 2 + u) * P
-                        nc.tensor.transpose(bank[:, b, u, :], words[:, first : first + P], ident[:])
+                        first_word = ((blocks * j + b) * 2 + u) * P
+                        nc.tensor.transpose(bank[:, b, u, :], words[:, first_word : first_word + P], ident[:])
                 copy = nc.vector.tensor_copy if (a == 1 and j == 1) else nc.scalar.copy
-                copy(pairs[:, 2 * j : 2 * j + 2], bank[:].rearrange("p b u t -> p b t u"))
+                copy(pairs[:, blocks * j : blocks * (j + 1)], bank[:].rearrange("p b u t -> p b t u"))
             z_bf[a, h] = grouped
 
         def quantise_z(a, h):
-            tag = "root7" if (a, h) == (0, 0) else "z_codes%d_%d" % (a, h)
+            tag = "root%d" % LAST if (a, h) == (0, 0) else "z_codes%d_%d" % (a, h)
             codes = keep.tile([P, BANK], U32, name="z_codes%d_%d" % (a, h), tag=tag, align_bytes=64)
             scales = keep.tile([P, BANK], U8, name="z_scales%d_%d" % (a, h), align_bytes=64)
-            nc.vector.quantize_mx(out=codes[:].bitcast(FP8X4), scales=scales[:], in_=z_bf[a, h][:])
+            width = BANK // 2 if (a, h) == (1, 0) else BANK
+            for t0 in range(0, BANK, width):
+                nc.vector.quantize_mx(
+                    out=codes[:, t0 : t0 + width].bitcast(FP8X4),
+                    scales=scales[:, t0 : t0 + width],
+                    in_=z_bf[a, h][:, t0 * PACK : (t0 + width) * PACK],
+                )
             z_q[a, h] = (codes, scales)
 
         y_ps = {}
-        y_tags = ["p0", "p1", "t1_0", "t1_1"] * 2
+        y_tags = ["p0", "p1", "sum0", "sum1"]
 
         def effort_pass(a, h, n):
             if a == 0:
-                y_ps[h, n] = psum.tile([P, BANK], F32, name="y_ps", tag=y_tags[4 * h + n])
+                y_ps[h, n] = psum.tile([P, BANK], F32, name="y_ps", tag=y_tags[n])
             codes, scales = z_q[a, h]
             nc.tensor.matmul_mx(
                 out=y_ps[h, n][:],
@@ -312,7 +313,7 @@ def tile_list_robot_contact_effort_kernel(
             nc.scalar.activation(result[:], y_ps[h, n][:], ACT.Square)
             nc.sync.dma_start(out[n * P : (n + 1) * P, h * BANK : (h + 1) * BANK], result[:])
 
-        for g in range(3):
+        for g in range(AHEAD + 1):
             round_w1(g)
             quantise_w1(g)
         response(0)
@@ -321,38 +322,36 @@ def tile_list_robot_contact_effort_kernel(
             scatter(0, part)
         response(1)
         weigh(1, 0)
-        if FIRST == 2:
-            round_w1(2)
-            quantise_w1(2)
-        if FIRST == 2:
-            round_w1(3)
-        quantise_w1(3)
+        quantise_w1(1 + AHEAD)
+
         for g in range(ROW_TILES):
             if g > 0:
                 scatter(g, 0)
-            if g + 2 < ROW_TILES:
-                response(g + 2)
-                weigh(g + 2, 0)
-            if g + 4 < ROW_TILES:
-                quantise_w1(g + 4)
-            if g >= LAG:
-                round_sums(g - LAG)
-            if g in (TB, TB + 1):
-                turn_back(0, g - TB)
-                quantise_z(0, g - TB)
+            coming = g + 2
+            if coming < ROW_TILES:
+                response(coming)
+                weigh(coming, 0)
+            if coming + AHEAD < ROW_TILES:
+                quantise_w1(coming + AHEAD)
+            if g > 0:
+                round_sums(g - 1)
+            if g in (LAST - 2, LAST - 1):
+                turn_back(0, g - (LAST - 2))
+                quantise_z(0, g - (LAST - 2))
             add_turned(g, state_sb[g], True)
-            if g == ROW_TILES - 1:
-                for n in range(4):
+            if g == LAST:
+                for n in range(OUT_TILES):
                     effort_pass(0, 0, n)
             add_turned(g, pages[g % 2], False)
-        for g in range(ROW_TILES - LAG, ROW_TILES):
-            round_sums(g)
+
+        round_sums(LAST)
         for h in range(HALVES):
             turn_back(1, h)
             quantise_z(1, h)
-        for h in range(HALVES):
-            for n in range(4):
-                if (h, n) not in y_ps:
-                    effort_pass(0, h, n)
-                effort_pass(1, h, n)
-                finish(h, n)
+        for n in range(OUT_TILES):
+            effort_pass(1, 0, n)
+            finish(0, n)
+        for n in range(OUT_TILES):
+            for a in range(PASSES):
+                effort_pass(a, 1, n)
+            finish(1, n)

from contextlib import ExitStack

import concourse.mybir as mybir
from concourse.masks import make_identity

K, T, S, H, T2, N = 1024, 2048, 512, 1024, 1024, 512
FLOPS = 2 * K * H * S + 2 * H * N * T2

F32 = mybir.dt.float32
BF16 = mybir.dt.bfloat16
I32 = mybir.dt.int32
U32 = mybir.dt.uint32
U16 = mybir.dt.uint16
U8 = mybir.dt.uint8
FP8X4 = mybir.dt.float8_e4m3fn_x4
FP4X4 = mybir.dt.float4_e2m1fn_x4
ACT = mybir.ActivationFunctionType
ALU = mybir.AluOpType

P = 128
PACK = 4
K_PASS = P * PACK
PASSES = 2
BANK = 512
QUADRANTS = 4
ROW_TILES = H // P
LAST = ROW_TILES - 1
HALVES = T2 // BANK
BLOCKS = BANK // P
OUT_TILES = N // P
RUN = P // PACK
AHEAD = 2
BEHIND = 3


def tile_list_robot_contact_effort_kernel(
    tc, tab_words, tab_scales, offs, w1, c, wgs, offs2, state, w4_words, w4_scales, out
):
    nc = tc.nc
    with ExitStack() as ctx:
        keep = ctx.enter_context(tc.tile_pool(name="keep", bufs=1))
        psum = ctx.enter_context(tc.psum_pool(name="psum", bufs=1))

        w1_raw, tab_w, state_sb = {}, [], {}

        def w1_tile(g0, count):
            raw = keep.tile([P, PASSES, PACK, count * P], F32, name="w1_raw%d" % g0)
            for j in range(count):
                w1_raw[g0 + j] = raw[:, :, :, j * P : (j + 1) * P]
            return raw

        def load_w1_pass(raw, a, g0, count):
            rows = w1[a * K_PASS : (a + 1) * K_PASS, g0 * P : (g0 + count) * P]
            nc.sync.dma_start(raw[:, a], rows.rearrange("(p i) c -> p i c", i=PACK))

        def load_w1(g0, count):
            raw = w1_tile(g0, count)
            for a in range(PASSES):
                load_w1_pass(raw, a, g0, count)

        def load_table(a):
            words = keep.tile([P, T], U32, name="tab_w%d" % a, align_bytes=64)
            nc.sync.dma_start(words[:].bitcast(I32), tab_words[a].rearrange("p t i -> p (t i)").bitcast(I32))
            tab_w.append(words)

        def load_state(g):
            rows = keep.tile([P, T2], F32, name="state%d" % g)
            nc.sync.dma_start(rows[:], state[g * P : (g + 1) * P, :])
            state_sb[g] = rows

        c_rows = keep.tile([P, P], F32, name="c_rows")
        tab_sc = keep.tile([P, T], U8, name="tab_sc", align_bytes=64)
        offs_sb = keep.tile([P, S // 16], U16, name="offs_sb")

        raw_first = w1_tile(0, 2)
        load_w1_pass(raw_first, 0, 0, 2)
        nc.gpsimd.memset(c_rows[:], 1.0)
        nc.sync.dma_start(c_rows[0:ROW_TILES, :], c.rearrange("(g q) -> g q", q=P))
        nc.vector.memset(tab_sc[:].bitcast(I32), 0)
        for q in range(QUADRANTS):
            nc.sync.dma_start(
                tab_sc[32 * q : 32 * q + 4 * PASSES, :].bitcast(I32), tab_scales[:, 4 * q : 4 * q + 4, :].bitcast(I32)
            )
        nc.sync.dma_start(offs_sb[:], offs)
        load_table(0)
        load_w1_pass(raw_first, 1, 0, 2)
        load_table(1)
        load_w1(2, 1)
        wgs_sb = keep.tile([P, S], F32, name="wgs_sb")
        nc.sync.dma_start(wgs_sb[:], wgs)
        offs2_sb = keep.tile([P, S // 16], U16, name="offs2_sb")
        nc.sync.dma_start(offs2_sb[:], offs2)
        load_w1(3, 1)
        load_state(0)
        load_w1(4, 2)
        load_state(1)
        load_w1(6, 2)
        load_state(2)
        load_state(3)
        w4_w = keep.tile([P, PASSES, 2 * N], U8, name="w4_w", align_bytes=64)
        nc.sync.dma_start(w4_w[:].bitcast(I32), w4_words.rearrange("a p n -> p a n").bitcast(I32))
        w4_sc = keep.tile([P, PASSES, N], U8, name="w4_sc", align_bytes=64)
        nc.vector.memset(w4_sc[:].bitcast(I32), 0)
        for q in range(QUADRANTS):
            nc.sync.dma_start(
                w4_sc[32 * q : 32 * q + 4].bitcast(I32),
                w4_scales[:, 4 * q : 4 * q + 4, :].rearrange("a r n -> r a n").bitcast(I32),
            )
        for g in range(4, ROW_TILES):
            load_state(g)

        ident = keep.tile([P, P], F32, name="ident")
        make_identity(nc, ident[:])
        pages = []
        for j in range(2):
            page = keep.tile([P, T2], F32, name="page%d" % j)
            nc.gpsimd.memset(page[:], 0.0)
            pages.append(page)

        c_ps = psum.tile([P, P], F32, name="c_ps", tag="back0")
        nc.tensor.transpose(c_ps[:], c_rows[:], ident[:])
        s_col = keep.tile([P, ROW_TILES], F32, name="s_col")
        nc.scalar.activation(s_col[:], c_ps[:, 0:ROW_TILES], ACT.Abs_reciprocal_sqrt)
        neg_s2 = keep.tile([P, ROW_TILES], F32, name="neg_s2")
        nc.vector.scalar_tensor_tensor(neg_s2[:], s_col[:], -1.0, s_col[:], ALU.mult, ALU.mult)
        cs2 = keep.tile([P, ROW_TILES], F32, name="cs2")
        nc.vector.scalar_tensor_tensor(cs2[:], c_ps[:, 0:ROW_TILES], -1.0, neg_s2[:], ALU.mult, ALU.mult)

        v_sc = keep.tile([P, S], U8, name="v_sc", align_bytes=64)
        v_w = [keep.tile([P, S], U32, name="v_w%d" % a, align_bytes=64) for a in range(PASSES)]
        nc.vector.tensor_copy(v_sc[:], tab_sc[:].indirect(offs_sb[:]))
        nc.vector.tensor_copy(v_w[0][:], tab_w[0][:].indirect(offs_sb[:]))
        for j0 in (0, S // 2):
            j1 = j0 + S // 2
            nc.vector.tensor_copy(v_w[1][:, j0:j1], tab_w[1][:].indirect(offs_sb[:, j0 // 16 : j1 // 16]))

        w1_bf, w1_q = {}, {}

        def round_w1(g):
            grouped = keep.tile([P, PASSES * P * PACK], BF16, name="w1_bf%d" % g, align_bytes=64)
            dst = grouped[:].rearrange("p (a c j i) -> p a c i j", a=PASSES, j=4, i=PACK)
            src = w1_raw[g].rearrange("p a i (c j) -> p a c i j", j=4)
            copy = nc.vector.tensor_copy if g in (0, 2) else nc.scalar.copy
            copy(dst, src)
            w1_bf[g] = grouped

        def quantise_w1(g):
            tag = "root%d" % (g - AHEAD) if g > AHEAD else "w1_codes%d" % g
            codes = keep.tile([P, PASSES * P], U32, name="w1_codes%d" % g, tag=tag, align_bytes=64)
            scales = keep.tile([P, PASSES * P], U8, name="w1_scales%d" % g, align_bytes=64)
            nc.vector.quantize_mx(out=codes[:].bitcast(FP8X4), scales=scales[:], in_=w1_bf[g][:])
            w1_q[g] = (codes, scales)

        z_turned = [keep.tile([P, T2 * PACK], BF16, name="z_turned%d" % a) for a in range(PASSES)]

        def room_of(g):
            a, quarter = divmod(g, PACK)
            words = z_turned[a][:].bitcast(F32).rearrange("t (r m) -> t r m", m=P)
            return words[:, :, RUN * quarter : RUN * (quarter + 1)]

        def runs(ap, length=RUN):
            return ap.rearrange("p (r m) -> p r m", m=length)

        def parts_of(g):
            if g == 0:
                return [("p0", 0, S // 2), ("back1", S // 2, S)]
            return [("p%d" % (g % 2), 0, S)]

        p_ps, recips, neg_h, sums = {}, {}, {}, {}
        start_scratch = keep.tile([P, 2 * S], F32, name="start_scratch")

        def response(g):
            codes, scales = w1_q[g]
            ahead = g + AHEAD if 0 < g < ROW_TILES - AHEAD else None
            if g == 0:
                root_of = {0: start_scratch[:, 128:384], S // 2: start_scratch[:, 768:1024]}
                sq_tile = keep.tile([P, S // 2], F32, name="sq0")
                sq_of = {0: runs(sq_tile[:]), S // 2: runs(start_scratch[:, 0:256])}
            else:
                root_tile = keep.tile([P, S], F32, name="root%d" % g, align_bytes=64)
                root_of = {0: root_tile[:]}
                if g == 1:
                    sq_of = {0: runs(start_scratch[:, 256:768])}
                elif g < BEHIND:
                    sq_tile = keep.tile([P, S], F32, name="sq%d" % g, tag="recip0")
                    sq_of = {0: runs(sq_tile[:])}
                else:
                    sq_of = {0: room_of(g - BEHIND)}
            if ahead:
                recip = w1_raw[ahead][:, 0]
            elif g < LAST:
                recip_tile = keep.tile([P, S], F32, name="recip%d" % g)
                recip = runs(recip_tile[:])
            else:
                recip = room_of(LAST - 1)
            for tag, j0, j1 in parts_of(g):
                bank = psum.tile([P, j1 - j0], F32, name="p_ps", tag=tag)
                p_ps[g, j0] = bank
                for a in range(PASSES):
                    cols = slice(a * P, (a + 1) * P)
                    nc.tensor.matmul_mx(
                        out=bank[:],
                        lhsT=codes[:, cols].bitcast(FP8X4),
                        lhsT_scale=scales[:, cols],
                        rhs=v_w[a][:, j0:j1].bitcast(FP8X4),
                        rhs_scale=v_sc[4 * a : P, j0:j1],
                        start=(a == 0),
                        stop=(a == PASSES - 1),
                    )
                nc.scalar.activation(sq_of[j0], runs(bank[:]), ACT.Square, scale=s_col[:, g : g + 1])
                nc.scalar.activation(runs(root_of[j0]), sq_of[j0], ACT.Abs_reciprocal_sqrt, bias=cs2[:, g : g + 1])
                if ahead:
                    round_w1(ahead)
                recips[g, j0] = recip[:, j0 // RUN : j1 // RUN] if g == 0 else recip
                nc.scalar.activation(recips[g, j0], runs(root_of[j0], recip.shape[2]), ACT.Square)

        def weigh(g, part):
            tag, j0, j1 = parts_of(g)[part]
            product = keep.tile([P, j1 - j0], F32, name="neg_h%d_%d" % (g, part))
            recip = recips[g, j0]
            length = recip.shape[2]
            nc.vector.scalar_tensor_tensor(
                runs(product[:], length), runs(p_ps[g, j0][:], length), neg_s2[:, g : g + 1], recip, ALU.mult, ALU.mult
            )
            neg_h[g, part] = product

        def scatter(g, part):
            tag, j0, j1 = parts_of(g)[part]
            nc.vector.tensor_tensor(
                pages[g % 2][:].indirect(offs2_sb[:, j0 // 16 : j1 // 16]), neg_h[g, part][:], wgs_sb[:, j0:j1], ALU.mult
            )

        def add_turned(g, source, opening):
            if opening:
                tags = ["sum%d" % (2 * (g % 2) + h) for h in range(HALVES)] + (["back0", "back1"] if g == LAST else [])
                sums[g] = [psum.tile([P, T2 // P // len(tags), P], F32, name="sum_ps", tag=tag) for tag in tags]
            blocks = T2 // P // len(sums[g])
            for j, bank in enumerate(sums[g]):
                for b in range(blocks):
                    cols = slice((j * blocks + b) * P, (j * blocks + b + 1) * P)
                    nc.tensor.matmul(
                        bank[:, b, :], source[:, cols], ident[:],
                        start=(opening and b == 0), stop=(not opening and b == blocks - 1), is_transpose=True,
                    )

        def round_sums(g):
            a, quarter = divmod(g, PACK)
            view = z_turned[a][:].rearrange("t (b u m e) -> t b u m e", u=2, m=P, e=2)
            blocks = T2 // P // len(sums[g])
            for j, bank in enumerate(sums[g]):
                copy = nc.vector.tensor_copy if (g == LAST and j % 2 == 1) else nc.scalar.copy
                copy(
                    view[:, j * blocks : (j + 1) * blocks, :, RUN * quarter : RUN * (quarter + 1), :],
                    bank[:].rearrange("t b (m u e) -> t b u m e", u=2, e=2),
                )

        z_bf, z_q = {}, {}
        back_tags = {
            (0, 0): ["back0", "back1"],
            (0, 1): ["back0", "back1"],
            (1, 0): ["sum2", "sum3", "back0", "back1"],
            (1, 1): ["sum2", "sum3"],
        }

        def turn_back(a, h):
            words = z_turned[a][:].bitcast(F32)[:, h * 2 * BANK : (h + 1) * 2 * BANK]
            tag = "root%d" % (LAST - 1) if (a, h) == (0, 0) else "z_bf%d_%d" % (a, h)
            grouped = keep.tile([P, BANK * PACK], BF16, name="z_bf%d_%d" % (a, h), tag=tag, align_bytes=64)
            pairs = grouped[:].bitcast(F32).rearrange("p (b t u) -> p b t u", t=P, u=2)
            blocks = BLOCKS // len(back_tags[a, h])
            for j, tag in enumerate(back_tags[a, h]):
                bank = psum.tile([P, blocks, 2, P], F32, name="back_ps", tag=tag)
                for b in range(blocks):
                    for u in range(2):
                        first_word = ((blocks * j + b) * 2 + u) * P
                        nc.tensor.transpose(bank[:, b, u, :], words[:, first_word : first_word + P], ident[:])
                copy = nc.vector.tensor_copy if (a == 1 and j == 1) else nc.scalar.copy
                copy(pairs[:, blocks * j : blocks * (j + 1)], bank[:].rearrange("p b u t -> p b t u"))
            z_bf[a, h] = grouped

        def quantise_z(a, h):
            tag = "root%d" % LAST if (a, h) == (0, 0) else "z_codes%d_%d" % (a, h)
            codes = keep.tile([P, BANK], U32, name="z_codes%d_%d" % (a, h), tag=tag, align_bytes=64)
            scales = keep.tile([P, BANK], U8, name="z_scales%d_%d" % (a, h), align_bytes=64)
            width = BANK // 2 if (a, h) == (1, 0) else BANK
            for t0 in range(0, BANK, width):
                nc.vector.quantize_mx(
                    out=codes[:, t0 : t0 + width].bitcast(FP8X4),
                    scales=scales[:, t0 : t0 + width],
                    in_=z_bf[a, h][:, t0 * PACK : (t0 + width) * PACK],
                )
            z_q[a, h] = (codes, scales)

        y_ps = {}
        y_tags = ["p0", "p1", "sum0", "sum1"]

        def effort_pass(a, h, n):
            if a == 0:
                y_ps[h, n] = psum.tile([P, BANK], F32, name="y_ps", tag=y_tags[n])
            codes, scales = z_q[a, h]
            nc.tensor.matmul_mx(
                out=y_ps[h, n][:],
                lhsT=w4_w[:, a, 2 * n * P : 2 * (n + 1) * P].bitcast(FP4X4),
                lhsT_scale=w4_sc[:, a, n * P : (n + 1) * P],
                rhs=codes[:].bitcast(FP8X4),
                rhs_scale=scales[:],
                start=(a == 0),
                stop=(a == PASSES - 1),
            )

        def finish(h, n):
            result = keep.tile([P, BANK], F32, name="result%d_%d" % (h, n))
            nc.scalar.activation(result[:], y_ps[h, n][:], ACT.Square)
            nc.sync.dma_start(out[n * P : (n + 1) * P, h * BANK : (h + 1) * BANK], result[:])

        for g in range(AHEAD + 1):
            round_w1(g)
            quantise_w1(g)
        response(0)
        for part in range(2):
            weigh(0, part)
            scatter(0, part)
        response(1)
        weigh(1, 0)
        quantise_w1(1 + AHEAD)

        for g in range(ROW_TILES):
            if g > 0:
                scatter(g, 0)
            coming = g + 2
            if coming < ROW_TILES:
                response(coming)
                weigh(coming, 0)
            if coming + AHEAD < ROW_TILES:
                quantise_w1(coming + AHEAD)
            if g > 0:
                round_sums(g - 1)
            if g in (LAST - 2, LAST - 1):
                turn_back(0, g - (LAST - 2))
                quantise_z(0, g - (LAST - 2))
            add_turned(g, state_sb[g], True)
            if g == LAST:
                for n in range(OUT_TILES):
                    effort_pass(0, 0, n)
            add_turned(g, pages[g % 2], False)

        round_sums(LAST)
        for h in range(HALVES):
            turn_back(1, h)
            quantise_z(1, h)
        for n in range(OUT_TILES):
            effort_pass(1, 0, n)
            finish(0, n)
        for n in range(OUT_TILES):
            for a in range(PASSES):
                effort_pass(a, 1, n)
            finish(1, n)
